import numpy as np
import ml_dtypes

BF16 = ml_dtypes.bfloat16


def bf(x):
    return np.asarray(x, np.float32).astype(BF16)


def f32(x):
    return np.asarray(x, np.float32)


def f64(x):
    return np.asarray(x).astype(np.float64)


def striped(idx):
    return np.tile(idx.reshape(-1, 16).T, (8, 1))


S, K, M, N, D, V = 1024, 128, 128, 384, 4, 96


def setup_inputs():
    return {"table": bf(np.random.standard_normal((K, S))), "w": bf(np.random.standard_normal((K, M)) / np.sqrt(K)), "b": f32(0.5 * np.random.standard_normal((M, 1))), "offs": striped(np.random.permutation(np.tile(np.arange(S), 2))[:N])}


def reference(table, w, b, offs):
    idx = offs[:16].T.reshape(-1)
    x = f64(table)[:, idx]
    y = f64(w).T @ x
    z = y + f64(b)
    return z.reshape(M, V, D).max(axis=2)

@@ -1,0 +1,42 @@
+import concourse.mybir as mybir
+
+BF16, F32, U16 = mybir.dt.bfloat16, mybir.dt.float32, mybir.dt.uint16
+
+K = 128
+S = 1024
+M = 128
+N = 384
+D = 4
+V = N // D
+
+FLOPS = 2 * K * M * N
+
+
+def tile_gather_matmul_kernel(tc, table, w, b, offs, out):
+    nc = tc.nc
+    with (
+        tc.tile_pool(name="held", bufs=1) as held,
+        tc.psum_pool(name="psum", bufs=1) as psum,
+    ):
+        offsets = held.tile([128, N // 16], U16, name="offsets")
+        nc.sync.dma_start(offsets[:], offs)
+        nodes = held.tile([K, S], BF16, name="nodes")
+        nc.sync.dma_start(nodes[:], table)
+        weights = held.tile([K, M], BF16, name="weights")
+        nc.scalar.dma_start(weights[:], w)
+        bias = held.tile([M, 1], F32, name="bias")
+        nc.scalar.dma_start(bias[:], b)
+
+        projected = psum.tile([M, N], F32, name="projected")
+        nc.tensor.matmul(projected[:], weights[:], nodes[:].indirect(offsets[:]), start=True, stop=True)
+
+        pooled = held.tile([M, V], F32, name="pooled")
+        nc.vector.tensor_reduce(
+            pooled[:],
+            projected[:].rearrange("m (v d) -> m v d", d=D),
+            axis=mybir.AxisListType.X,
+            op=mybir.AluOpType.max,
+        )
+        result = held.tile([M, V], F32, name="result")
+        nc.vector.tensor_scalar_add(result[:], pooled[:], bias[:, 0:1])
+        nc.sync.dma_start(out, result[:])

@@ -11,6 +11,9 @@ V = N // D
 
 FLOPS = 2 * K * M * N
 
+PIECES = 2
+Q = N // PIECES
+
 
 def tile_gather_matmul_kernel(tc, table, w, b, offs, out):
     nc = tc.nc
@@ -27,16 +30,17 @@ def tile_gather_matmul_kernel(tc, table, w, b, offs, out):
         bias = held.tile([M, 1], F32, name="bias")
         nc.scalar.dma_start(bias[:], b)
 
-        projected = psum.tile([M, N], F32, name="projected")
-        nc.tensor.matmul(projected[:], weights[:], nodes[:].indirect(offsets[:]), start=True, stop=True)
-
         pooled = held.tile([M, V], F32, name="pooled")
-        nc.vector.tensor_reduce(
-            pooled[:],
-            projected[:].rearrange("m (v d) -> m v d", d=D),
-            axis=mybir.AxisListType.X,
-            op=mybir.AluOpType.max,
-        )
+        for p in range(PIECES):
+            projected = psum.tile([M, Q], F32, name=f"projected{p}")
+            picked = nodes[:].indirect(offsets[:, p * (Q // 16) : (p + 1) * (Q // 16)])
+            nc.tensor.matmul(projected[:], weights[:], picked, start=True, stop=True)
+            nc.vector.tensor_reduce(
+                pooled[:, p * (Q // D) : (p + 1) * (Q // D)],
+                projected[:].rearrange("m (v d) -> m v d", d=D),
+                axis=mybir.AxisListType.X,
+                op=mybir.AluOpType.max,
+            )
         result = held.tile([M, V], F32, name="result")
         nc.vector.tensor_scalar_add(result[:], pooled[:], bias[:, 0:1])
         nc.sync.dma_start(out, result[:])

@@ -13,6 +13,8 @@ FLOPS = 2 * K * M * N
 
 PIECES = 2
 Q = N // PIECES
+WARMING = 6
+WIDTH = 256
 
 
 def tile_gather_matmul_kernel(tc, table, w, b, offs, out):
@@ -29,6 +31,12 @@ def tile_gather_matmul_kernel(tc, table, w, b, offs, out):
         nc.scalar.dma_start(weights[:], w)
         bias = held.tile([M, 1], F32, name="bias")
         nc.scalar.dma_start(bias[:], b)
+
+        zeros = held.tile([K, WIDTH], BF16, name="zeros")
+        nc.vector.memset(zeros[:], 0.0)
+        unread = psum.tile([M, WIDTH], F32, name="unread")
+        for r in range(WARMING):
+            nc.tensor.matmul(unread[:], zeros[:, 0:M], zeros[:], start=True, stop=True)
 
         pooled = held.tile([M, V], F32, name="pooled")
         for p in range(PIECES):

@@ -11,8 +11,7 @@ V = N // D
 
 FLOPS = 2 * K * M * N
 
-PIECES = 2
-Q = N // PIECES
+WIDTHS = (256, 128)
 WARMING = 6
 WIDTH = 256
 
@@ -23,14 +22,14 @@ def tile_gather_matmul_kernel(tc, table, w, b, offs, out):
         tc.tile_pool(name="held", bufs=1) as held,
         tc.psum_pool(name="psum", bufs=1) as psum,
     ):
+        nodes = held.tile([K, S], BF16, name="nodes")
+        nc.scalar.dma_start(nodes[:], table)
         offsets = held.tile([128, N // 16], U16, name="offsets")
         nc.sync.dma_start(offsets[:], offs)
-        nodes = held.tile([K, S], BF16, name="nodes")
-        nc.sync.dma_start(nodes[:], table)
         weights = held.tile([K, M], BF16, name="weights")
-        nc.scalar.dma_start(weights[:], w)
+        nc.sync.dma_start(weights[:], w)
         bias = held.tile([M, 1], F32, name="bias")
-        nc.scalar.dma_start(bias[:], b)
+        nc.sync.dma_start(bias[:], b)
 
         zeros = held.tile([K, WIDTH], BF16, name="zeros")
         nc.vector.memset(zeros[:], 0.0)
@@ -39,16 +38,20 @@ def tile_gather_matmul_kernel(tc, table, w, b, offs, out):
             nc.tensor.matmul(unread[:], zeros[:, 0:M], zeros[:], start=True, stop=True)
 
         pooled = held.tile([M, V], F32, name="pooled")
-        for p in range(PIECES):
-            projected = psum.tile([M, Q], F32, name=f"projected{p}")
-            picked = nodes[:].indirect(offsets[:, p * (Q // 16) : (p + 1) * (Q // 16)])
+        first = 0
+        for p, width in enumerate(WIDTHS):
+            projected = psum.tile([M, width], F32, name=f"projected{p}")
+            picked = nodes[:].indirect(offsets[:, first // 16 : (first + width) // 16])
             nc.tensor.matmul(projected[:], weights[:], picked, start=True, stop=True)
             nc.vector.tensor_reduce(
-                pooled[:, p * (Q // D) : (p + 1) * (Q // D)],
+                pooled[:, first // D : (first + width) // D],
                 projected[:].rearrange("m (v d) -> m v d", d=D),
                 axis=mybir.AxisListType.X,
                 op=mybir.AluOpType.max,
             )
+            first += width
         result = held.tile([M, V], F32, name="result")
         nc.vector.tensor_scalar_add(result[:], pooled[:], bias[:, 0:1])
-        nc.sync.dma_start(out, result[:])
+        cut = WIDTHS[0] // D
+        nc.scalar.dma_start(out[:, 0:cut], result[:, 0:cut])
+        nc.sync.dma_start(out[:, cut:V], result[:, cut:V])

@@ -12,8 +12,6 @@ V = N // D
 FLOPS = 2 * K * M * N
 
 WIDTHS = (256, 128)
-WARMING = 6
-WIDTH = 256
 
 
 def tile_gather_matmul_kernel(tc, table, w, b, offs, out):
@@ -30,12 +28,6 @@ def tile_gather_matmul_kernel(tc, table, w, b, offs, out):
         nc.sync.dma_start(weights[:], w)
         bias = held.tile([M, 1], F32, name="bias")
         nc.sync.dma_start(bias[:], b)
-
-        zeros = held.tile([K, WIDTH], BF16, name="zeros")
-        nc.vector.memset(zeros[:], 0.0)
-        unread = psum.tile([M, WIDTH], F32, name="unread")
-        for r in range(WARMING):
-            nc.tensor.matmul(unread[:], zeros[:, 0:M], zeros[:], start=True, stop=True)
 
         pooled = held.tile([M, V], F32, name="pooled")
         first = 0

@@ -11,7 +11,8 @@ V = N // D
 
 FLOPS = 2 * K * M * N
 
-WIDTHS = (256, 128)
+WIDTHS = (128, 128, 128)
+CUT = 64
 
 
 def tile_gather_matmul_kernel(tc, table, w, b, offs, out):
@@ -44,6 +45,5 @@ def tile_gather_matmul_kernel(tc, table, w, b, offs, out):
             first += width
         result = held.tile([M, V], F32, name="result")
         nc.vector.tensor_scalar_add(result[:], pooled[:], bias[:, 0:1])
-        cut = WIDTHS[0] // D
-        nc.scalar.dma_start(out[:, 0:cut], result[:, 0:cut])
-        nc.sync.dma_start(out[:, cut:V], result[:, cut:V])
+        nc.scalar.dma_start(out[:, 0:CUT], result[:, 0:CUT])
+        nc.sync.dma_start(out[:, CUT:V], result[:, CUT:V])

@@ -12,7 +12,6 @@ V = N // D
 FLOPS = 2 * K * M * N
 
 WIDTHS = (128, 128, 128)
-CUT = 64
 
 
 def tile_gather_matmul_kernel(tc, table, w, b, offs, out):
@@ -45,5 +44,4 @@ def tile_gather_matmul_kernel(tc, table, w, b, offs, out):
             first += width
         result = held.tile([M, V], F32, name="result")
         nc.vector.tensor_scalar_add(result[:], pooled[:], bias[:, 0:1])
-        nc.scalar.dma_start(out[:, 0:CUT], result[:, 0:CUT])
-        nc.sync.dma_start(out[:, CUT:V], result[:, CUT:V])
+        nc.sync.dma_start(out, result[:])

@@ -22,10 +22,10 @@ def tile_gather_matmul_kernel(tc, table, w, b, offs, out):
     ):
         nodes = held.tile([K, S], BF16, name="nodes")
         nc.scalar.dma_start(nodes[:], table)
-        offsets = held.tile([128, N // 16], U16, name="offsets")
-        nc.sync.dma_start(offsets[:], offs)
         weights = held.tile([K, M], BF16, name="weights")
         nc.sync.dma_start(weights[:], w)
+        offsets = held.tile([128, N // 16], U16, name="offsets")
+        nc.sync.dma_start(offsets[:], offs)
         bias = held.tile([M, 1], F32, name="bias")
         nc.sync.dma_start(bias[:], b)
 

@@ -1,6 +1,7 @@
 import concourse.mybir as mybir
 
 BF16, F32, U16 = mybir.dt.bfloat16, mybir.dt.float32, mybir.dt.uint16
+IDENTITY = mybir.ActivationFunctionType.Identity
 
 K = 128
 S = 1024
@@ -29,19 +30,25 @@ def tile_gather_matmul_kernel(tc, table, w, b, offs, out):
         bias = held.tile([M, 1], F32, name="bias")
         nc.sync.dma_start(bias[:], b)
 
+        zeros = held.tile([M, 1], F32, name="zeros")
+        nc.vector.memset(zeros[:], 0.0)
+        unused = held.tile([M, 1], F32, name="unused")
+        nc.scalar.activation(unused[:], zeros[:], IDENTITY)
+
         pooled = held.tile([M, V], F32, name="pooled")
+        result = held.tile([M, V], F32, name="result")
         first = 0
         for p, width in enumerate(WIDTHS):
             projected = psum.tile([M, width], F32, name=f"projected{p}")
             picked = nodes[:].indirect(offsets[:, first // 16 : (first + width) // 16])
             nc.tensor.matmul(projected[:], weights[:], picked, start=True, stop=True)
+            columns = slice(first // D, (first + width) // D)
             nc.vector.tensor_reduce(
-                pooled[:, first // D : (first + width) // D],
+                pooled[:, columns],
                 projected[:].rearrange("m (v d) -> m v d", d=D),
                 axis=mybir.AxisListType.X,
                 op=mybir.AluOpType.max,
             )
+            nc.scalar.activation(result[:, columns], pooled[:, columns], IDENTITY, bias=bias[:, 0:1])
             first += width
-        result = held.tile([M, V], F32, name="result")
-        nc.vector.tensor_scalar_add(result[:], pooled[:], bias[:, 0:1])
-        nc.sync.dma_start(out, result[:])
+        nc.scalar.dma_start(out, result[:])

@@ -36,19 +36,23 @@ def tile_gather_matmul_kernel(tc, table, w, b, offs, out):
         nc.scalar.activation(unused[:], zeros[:], IDENTITY)
 
         pooled = held.tile([M, V], F32, name="pooled")
-        result = held.tile([M, V], F32, name="result")
         first = 0
         for p, width in enumerate(WIDTHS):
             projected = psum.tile([M, width], F32, name=f"projected{p}")
             picked = nodes[:].indirect(offsets[:, first // 16 : (first + width) // 16])
             nc.tensor.matmul(projected[:], weights[:], picked, start=True, stop=True)
-            columns = slice(first // D, (first + width) // D)
             nc.vector.tensor_reduce(
-                pooled[:, columns],
+                pooled[:, first // D : (first + width) // D],
                 projected[:].rearrange("m (v d) -> m v d", d=D),
                 axis=mybir.AxisListType.X,
                 op=mybir.AluOpType.max,
             )
-            nc.scalar.activation(result[:, columns], pooled[:, columns], IDENTITY, bias=bias[:, 0:1])
             first += width
-        nc.scalar.dma_start(out, result[:])
+
+        early = (N - WIDTHS[-1]) // D
+        early_result = held.tile([M, early], F32, name="early_result")
+        nc.scalar.activation(early_result[:], pooled[:, 0:early], IDENTITY, bias=bias[:, 0:1])
+        nc.scalar.dma_start(out[:, 0:early], early_result[:])
+        late_result = held.tile([M, V - early], F32, name="late_result")
+        nc.vector.tensor_scalar_add(late_result[:], pooled[:, early:V], bias[:, 0:1])
+        nc.sync.dma_start(out[:, early:V], late_result[:])

@@ -49,7 +49,7 @@ def tile_gather_matmul_kernel(tc, table, w, b, offs, out):
             )
             first += width
 
-        early = (N - WIDTHS[-1]) // D
+        early = WIDTHS[0] // D
         early_result = held.tile([M, early], F32, name="early_result")
         nc.scalar.activation(early_result[:], pooled[:, 0:early], IDENTITY, bias=bias[:, 0:1])
         nc.scalar.dma_start(out[:, 0:early], early_result[:])

import concourse.mybir as mybir

BF16, F32, U16 = mybir.dt.bfloat16, mybir.dt.float32, mybir.dt.uint16
IDENTITY = mybir.ActivationFunctionType.Identity

K = 128
S = 1024
M = 128
N = 384
D = 4
V = N // D

FLOPS = 2 * K * M * N

WIDTHS = (128, 128, 128)


def tile_gather_matmul_kernel(tc, table, w, b, offs, out):
    nc = tc.nc
    with (
        tc.tile_pool(name="held", bufs=1) as held,
        tc.psum_pool(name="psum", bufs=1) as psum,
    ):
        nodes = held.tile([K, S], BF16, name="nodes")
        nc.scalar.dma_start(nodes[:], table)
        weights = held.tile([K, M], BF16, name="weights")
        nc.sync.dma_start(weights[:], w)
        offsets = held.tile([128, N // 16], U16, name="offsets")
        nc.sync.dma_start(offsets[:], offs)
        bias = held.tile([M, 1], F32, name="bias")
        nc.sync.dma_start(bias[:], b)

        zeros = held.tile([M, 1], F32, name="zeros")
        nc.vector.memset(zeros[:], 0.0)
        unused = held.tile([M, 1], F32, name="unused")
        nc.scalar.activation(unused[:], zeros[:], IDENTITY)

        pooled = held.tile([M, V], F32, name="pooled")
        first = 0
        for p, width in enumerate(WIDTHS):
            projected = psum.tile([M, width], F32, name=f"projected{p}")
            picked = nodes[:].indirect(offsets[:, first // 16 : (first + width) // 16])
            nc.tensor.matmul(projected[:], weights[:], picked, start=True, stop=True)
            nc.vector.tensor_reduce(
                pooled[:, first // D : (first + width) // D],
                projected[:].rearrange("m (v d) -> m v d", d=D),
                axis=mybir.AxisListType.X,
                op=mybir.AluOpType.max,
            )
            first += width

        early = WIDTHS[0] // D
        early_result = held.tile([M, early], F32, name="early_result")
        nc.scalar.activation(early_result[:], pooled[:, 0:early], IDENTITY, bias=bias[:, 0:1])
        nc.scalar.dma_start(out[:, 0:early], early_result[:])
        late_result = held.tile([M, V - early], F32, name="late_result")
        nc.vector.tensor_scalar_add(late_result[:], pooled[:, early:V], bias[:, 0:1])
        nc.sync.dma_start(out[:, early:V], late_result[:])
